import numpy as np, ml_dtypes
CORES = [3,11,19,27,35,43,51,59]
N = 8
import mx_ref
BF = ml_dtypes.bfloat16
def gentries(a):
    return np.ascontiguousarray(a.reshape(8, 16, -1).transpose(0, 2, 1)).reshape(8, -1)
def gtable(e):
    e = np.asarray(e); return np.ascontiguousarray(e.reshape(8, -1, 16).transpose(0, 2, 1)).reshape(128, -1).astype(np.int32)
def gcols(t, e):
    v = np.concatenate([t.reshape(8, 16, -1, 4), np.zeros((8, 16, 1, 4), BF)], axis=2)
    return np.ascontiguousarray(np.stack([v[g][:, e[g]] for g in range(8)])).reshape(128, -1)
def tile(rs):
    return np.stack(rs, axis=2).reshape(128, -1).astype(BF)
def cut(t, i, w=512):
    return t[:, w * i:w * i + w]
def pick(q, e):
    c = np.concatenate([q[0].reshape(128, -1, 4), np.zeros((128, 1, 4), np.uint8)], axis=1); s = np.concatenate([q[1], np.ones((16, 1), np.uint8)], axis=1)
    return (np.ascontiguousarray(c[:, e].reshape(128, -1)), np.ascontiguousarray(s[:, e]))
def join(*qs):
    return (np.concatenate([q[0] for q in qs], axis=1), np.concatenate([q[1] for q in qs], axis=1))
def put(q, e, v):
    c, s = q[0].reshape(128, -1, 4).copy(), q[1].copy(); c[:, e] = v[0].reshape(128, -1, 4); s[:, e] = v[1]
    return (c.reshape(128, -1), s)
def pk(c, s):
    return (np.ascontiguousarray(c), mx_ref.live(s))
def emit(q):
    return q[0], q[1]
def packed(v, rng):
    q = [mx_ref.quantize(np.ascontiguousarray(v[r])) for r in range(N)]
    return np.stack([a for a, b in q]), np.stack([mx_ref.plane(b, rng) for a, b in q])
def values_of_codes():
    e, c = np.zeros((128, 128, 4), np.float32), np.zeros((128, 2, 4), np.uint8)
    e[np.arange(128), np.arange(128), 0] = 1
    c[:127, :, 0] = np.arange(256).reshape(2, 128).T[:127]
    return mx_ref.matmul(mx_ref.quantize(e.reshape(128, 512).astype(BF)), (c.reshape(128, 8), np.full((16, 2), 127, np.uint8))).T.reshape(-1).astype(np.float64)
CODE_VALUE, SCALE_VALUE = values_of_codes(), 2.0 ** (np.arange(256) - 127.0)
def decode(q):
    return (CODE_VALUE[q[0]].reshape(16, 8, -1, 4) * SCALE_VALUE[q[1]][:, None, :, None] + 0.0).reshape(128, -1).astype(np.float32)
def f(rng, *shape):
    return mx_ref.flush((rng.standard_normal(shape, dtype=np.float32) * np.exp2(rng.integers(-2, 3, shape[:-1] + (1,)))).astype(BF))
def wide(rng, *shape, cols=0):
    v = rng.standard_normal(shape, dtype=np.float32) * np.exp2(rng.integers(-12, 13, shape)).astype(np.float32)
    if cols: v *= np.repeat(np.exp2(rng.integers(-cols, cols + 1, shape[:-2] + (1, shape[-1] // 4))) * (rng.random(shape[:-2] + (1, shape[-1] // 4)) > 0.0625), 4, axis=-1).astype(np.float32)
    return mx_ref.flush(v.astype(BF))
C, P, E, T, R = 384, 32, 3, 96, 3
STEP = [1, 2, 4]
OPPOSITE = np.array([E * (P - 1 - q) + i for q in range(P) for i in range(E)])
def sow(n, s):
    o, m = np.zeros((8, C), int), np.zeros((8, P), int)
    for g in range(8):
        end = np.cumsum(n[g])
        mark = np.where(n[g] > 0, s[g][np.maximum(end - 1, 0)] + np.float32(0.0), np.float32(-np.inf))
        chosen = 4 * np.arange(P // 4) + np.argmax(mark.reshape(-1, 4), axis=1)
        pit = np.repeat(np.arange(P), n[g])
        k = np.arange(C) - (end - n[g])[pit]
        moved = np.isin(pit, chosen)
        to = np.where(moved, (pit + 1 + k) % P, pit)
        o[g] = np.lexsort((k, moved, to))
        m[g] = np.bincount(to, minlength=P)
    return o, m
def ends(n):
    i = np.arange(E)
    return np.where(i < n[:, :, None], np.cumsum(n, axis=1)[:, :, None] - 1 - i, -1).reshape(8, T)
def gput(t, e, h):
    a, b = t.reshape(8, 16, -1, 4).copy(), h.reshape(8, 16, -1, 4)
    for g in range(8):
        j = np.flatnonzero(e[g] >= 0)
        a[g][:, e[g][j]] = b[g][:, j]
    return a.reshape(128, -1)
def big(v):
    v = v.astype(np.float32)
    v[np.abs(v) < np.float32(2.0 ** -16)] = 0
    return v.astype(BF)
def numbers_of(rng):
    return {"x": big(f(rng, N, 128, 4 * C)), "u": np.array(f(rng, N, 128, 512)), "v": np.array(f(rng, N, 128, 512))}
def weights(rng, still=[]):
    w = big(f(rng, N, 128, 2048)).reshape(N, 8, 16, 4, 8, 16, 4)
    for i in still:
        w[:, :, i] = 0
        w[:, :, :, :, :, i] = 0
    c, p = packed(w.reshape(N, 128, 2048), rng)
    return {"wc": c, "ws": p}
def sizes(rng):
    n = np.zeros((N, 8, P), int)
    for r in range(N):
        for g in range(8):
            m = rng.integers(0, P, P)
            n[r, g] = np.bincount(m[rng.integers(0, P, C)], minlength=P)
    return n
def stored(n):
    return np.stack([gtable(a) for a in n])
def signs(rng):
    return np.stack([rng.permutation(8) % 2 * 2.0 - 1.0 for r in range(N)])
def setup_inputs(rng):
    return {**numbers_of(rng), **weights(rng), "sz": stored(sizes(rng))}
def setup_inputs_ties(rng):
    d = numbers_of(rng)
    e = rng.permutation(N)
    x = d["x"].reshape(N, 8, 16, C, 4)
    for r in range(N):
        k = np.zeros(C, int) if r == e[0] else rng.permutation(C) % 3
        a = x[r][:, :8, :3].copy()
        a[:, :, 2] = 0
        x[r][:, :8] = a[:, :, k]
    x[e[1]] = 0
    u = d["u"].reshape(N, 8, 16, 8, 16, 4)
    k = u.copy()
    u[:, :, :, :, 0] = 0
    for g in range(8): u[:, g, :8, g, 0] = k[:, g, :8, g, 0]
    return {"x": x.reshape(N, 128, 4 * C), "u": u.reshape(N, 128, 512), "v": d["v"], **weights(rng, range(8)), "sz": stored(sizes(rng))}
def setup_inputs_near(rng):
    d = numbers_of(rng)
    n = sizes(rng)
    x = d["x"].astype(np.float32).reshape(N, 8, 16, C, 4)
    x[:, :, 0] = 0
    x[:, :, 8:] = 0
    u = d["u"].reshape(N, 128, 128, 4)
    u[:, :, ::16] = 0
    o, c = rng.permutation(N) % 4, signs(rng)
    for r in range(N):
        if o[r] == 3:
            x[r, :, 9:] = rng.integers(8, 16, (8, 7, C, 4)) * 2.0 ** -30
            x[r, :, 9] = 0
            stays = rng.permutation(8) < 4
            for g in range(8):
                h, m = int(rng.integers(1, 5)), 4 * int(rng.integers(0, P // 4))
                if stays[g]: h = 1
                n[r, g] = 0
                n[r, g, m] = h
                n[r, g, m + 1 if stays[g] else m + 3] = C - h
                s = rng.integers(8, 10, C)
                s[h - 1], s[C - 1] = (9, 8) if stays[g] else (8, 9)
                x[r, g, 8, :, 0] = s * 2.0 ** -30
        else:
            size = 1.0 if o[r] < 2 else 2.0 ** -4
            s = (np.arange(C) + rng.integers(0, C, (8, 1))) % C // 8
            z = ((s[:, :, None] >> np.arange(8)) & 1) * np.exp2(np.arange(8) - 23.0) * size
            if o[r] < 2: x[r, :, 0, :, 0] = c[r][:, None]
            x[r, :, 8] = z[:, :, :4]
            x[r, :, 9] = z[:, :, 4:]
            x[r, :, 10:] = rng.integers(4, 8, (8, 6, C, 4)) * 2.0 ** -20 * size
        k = 1.0 if o[r] == 0 else 2.0 ** -30
        for h in range(0, 128, 16):
            u[r, h, h, 0] = k
            u[r, h + 8:h + 10, h] = k
    return {"x": x.reshape(N, 128, 4 * C).astype(BF), "u": u.reshape(N, 128, 512), "v": d["v"], **weights(rng, [0, 8, 9, 10, 11, 12, 13, 14, 15]), "sz": stored(n)}
def setup_inputs_huge(rng):
    d = numbers_of(rng)
    n = sizes(rng)
    c = np.stack([rng.permutation(C) % 2 * 2.0 - 1.0 for r in range(N)])
    r, z = np.arange(N), int(rng.integers(N))
    one = np.isin(r, [z] + [z ^ s for s in STEP])
    c[one] = ((r ^ (r >> 1) ^ (r >> 2)) % 2 * 2.0 - 1.0)[one][:, None]
    k = rng.random((N, 128, C, 4))
    x = 2.0 ** 30 * np.where(one[:, None, None, None], 0.75 + 0.125 * k, 0.08 + 0.01 * k) * c[:, None, :, None]
    x[z, :, C - 1] = 2.0 ** 30 * c[z, C - 1]
    for m in n[z]:
        m[P - 1] = np.sum(m[P - 4:])
        m[P - 4:P - 1] = 0
        m[np.argmax(m)] -= 1
        m[P - 1] += 1
    u = d["u"].reshape(N, 128, 128, 4)
    a = 2.0 ** 30 * (1 - 0.1 * rng.random((N, 128, 8, 4))) * signs(rng)[:, None, :, None]
    a[z] = 2.0 ** 30 * np.sign(a[z])
    u[:, :, ::16] = a.astype(np.float32).astype(BF)
    w = np.zeros((N, 128, 4, 128, 4), np.float32)
    i = np.arange(128)
    for b in range(4): w[:, i, b, i, b] = -1
    wc, ws = packed(w.reshape(N, 128, 2048).astype(BF), rng)
    return {"x": x.astype(np.float32).reshape(N, 128, 4 * C).astype(BF), "u": u.reshape(N, 128, 512), "v": d["v"], "wc": wc, "ws": ws, "sz": stored(n)}
def setup_inputs_pits(rng):
    d = setup_inputs(rng)
    n = np.zeros((N, 8, P), int)
    for r in range(N):
        k = rng.permutation(8)
        for g in range(8):
            m = n[r, g]
            q = 4 * rng.permutation(P // 4) + rng.integers(0, 4, P // 4)
            if k[g] == 0: m[q[0]] = C
            if k[g] == 1: m[P - 1] = C
            if k[g] == 2:
                m[q[:3]] = P - 1, P, P + 1
                m += np.bincount(4 * (q[3:] // 4)[rng.integers(0, P // 4 - 3, C - 3 * P)] + rng.integers(0, 4, C - 3 * P), minlength=P)
            if k[g] == 3 and r % 2 == 0: m += np.bincount(q[np.arange(C) % (P // 4)], minlength=P)
            if k[g] == 3 and r % 2 == 1:
                i = int(rng.integers(0, P // 4))
                m[3::4] = 4 * ((i - 1 - np.arange(P // 4)) % (P // 4)) + 1
                m[4 * (q[0] // 4) + 3] += C - np.sum(m)
            if k[g] == 4: m += np.bincount(np.arange(C) % P, minlength=P)
            if k[g] == 5:
                m[:] = rng.permutation(np.arange(P) % (E + 2))
                m[q[0]] += C - np.sum(m)
            if k[g] == 6: m[q[:2]] = C - 1, 1
            if k[g] == 7: m[q[:2]] = 2 * P, C - 2 * P
    d["sz"] = stored(n)
    return d
def setup_inputs_spread(rng):
    d = setup_inputs(rng)
    d["x"] = big(wide(rng, N, 128, 4 * C, cols=6))
    return d
def check_inputs(d):
    b = []
    for k in ("x", "u", "v"):
        a = np.abs(d[k].astype(np.float32))
        if not (np.isfinite(a).all() and ((a == 0) | (a >= 2.0 ** -30) & (a <= 2.0 ** 30)).all()): b.append("a value of " + k)
    if ((d["wc"] & 0x7F) == 0x7F).any(): b.append("a code of wc that is no number")
    z = np.zeros((128, 4, 4), np.float32)
    z[:, 1] = 2.0 ** -30
    z[:, 2] = 2.0 ** 30
    c, s = emit(mx_ref.quantize(z.reshape(128, 16).astype(BF)))
    for r in range(N):
        p = mx_ref.live(d["ws"][r])
        if not ((p == s[0, 0]) | (p >= s[0, 1]) & (p <= s[0, 2])).all(): b.append("a scale of ws")
        n = gentries(d["sz"][r]).astype(np.int64)
        if (n < 0).any(): b.append("a size of sz below 0")
        if (np.sum(n, axis=1) != C).any(): b.append("the sum of a group's sizes")
    return b
def reference(x, u, v, wc, ws, sz):
    qu = [mx_ref.quantize(u[r]) for r in range(N)]
    lay = [pk(wc[r], ws[r]) for r in range(N)]
    now = [x[r] for r in range(N)]
    n = [gentries(sz[r]) for r in range(N)]
    for t in range(R):
        own, sent = [], []
        for r in range(N):
            o, n[r] = sow(n[r], mx_ref.matmul(qu[r], mx_ref.quantize(now[r]))[::16])
            now[r] = gcols(now[r], o)
            own.append(gcols(now[r], ends(n[r])))
            sent.append(mx_ref.quantize(own[r]))
        came = decode(join(*sent))
        for r in range(N):
            c = cut(came, r ^ STEP[t], 4 * T).reshape(128, T, 4)[:, OPPOSITE].reshape(128, 4 * T)
            q = mx_ref.quantize((own[r].astype(np.float32) + c).astype(BF))
            h = tile([mx_ref.matmul(pick(lay[r], np.arange(128 * b, 128 * b + 128)), q) * np.float32(0.015625) + own[r][:, b::4].astype(np.float32) for b in range(4)])
            now[r] = gput(now[r], ends(n[r]), h)
    y, oz = np.zeros((N, 128, C), np.float32), np.zeros((N, 8, P), np.float32)
    oc, osc = np.zeros((N, 128, 4 * C), np.uint8), np.zeros((N, 16, C), np.uint8)
    for r in range(N):
        q = mx_ref.quantize(now[r])
        y[r] = mx_ref.matmul(mx_ref.quantize(v[r]), q)
        oz[r] = n[r]
        oc[r], osc[r] = emit(q)
    return {"y": y, "oz": oz, "oc": oc, "osc": osc}

from concourse.mybir import dt, AluOpType as OP, ActivationFunctionType as AF

C, P, E, TT, R = 384, 32, 3, 96, 3
PW = 496
ZERO = 480
KEY = 4097.0
BASE = [2.0 ** 20, 2.0 ** 20 + 2.0 ** 22]
STAY = 2.0 ** 22
PAD = 64528.0
HALF = -0.5 + 1.0 / 64
WHOLE = 1.5 * 2.0 ** 23
GUESS = [(80.0, 2200.0, 3600.0, 1.0, 1.0, 1.0), (150.0, 1800.0, 5000.0, 0.9, 0.8, 0.6), (60.0, 2800.0, 3000.0, 1.15, 1.3, 1.5)]
TRIES = 1000

F32 = [("iota", 480), ("mask", 384), ("seg", 384), ("one", 384), ("rcol", 1), ("crep", 192), ("cmsk", 192), ("cscan", 192),
       ("pat", 40), ("big", 72), ("pit", 81), ("pq", 80), ("dP", 40), ("levi", 32), ("nq", 32), ("p9", 32),
       ("thr", 16), ("dum", 16), ("i1", 32), ("ev", 32), ("jd", 24), ("qh", 2),
       ("S", 392), ("lk", 384), ("ls", 384), ("O", 576), ("om", 384), ("os", 384), ("es2", 384), ("ep", 384), ("yo", 384),
       ("lst", 8), ("NF", 40), ("VF", 56), ("Vk", 88), ("En", 72), ("D", 104), ("Rr", 120), ("lev", 64), ("Mn", 40), ("sub", 16), ("Cw", 200),
       ("M5", 48), ("Sf", 40), ("u", 40), ("DF", 40), ("DP", 40), ("ne", 32), ("cc", 2), ("fg", 2),
       ("cand", 64), ("T3", 192), ("cx", 16), ("cs", 16), ("arr", 2),
       ("em", 32), ("es", 32), ("inv", 16), ("pos", 16), ("tt", 16), ("off", 16), ("kp0", 6),
       ("RL", 192), ("AB", 192), ("EQ", 192), ("KQ", 192), ("fw", 192), ("W", 24), ("nW", 24), ("Wb", 24), ("cd", 24), ("idx", 24),
       ("x", 24), ("t3", 24), ("d", 24), ("N", 416), ("enc", 24), ("pm", 24), ("a5", 24), ("pf", 24), ("p1", 24), ("yp", 24), ("kf", 24),
       ("y", 24), ("y0", 24), ("lm", 24), ("l0", 24), ("l32", 24), ("q40", 24), ("kq", 24), ("km", 80), ("kt", 80), ("dK", 80), ("dF", 40)]
I32 = [("sz", 2), ("pc", 1), ("ri", 1), ("r1", 1), ("pi", 24), ("Ti", 6), ("Ta", 6), ("w", 80), ("w2", 80)]
U16 = [("cl", 16), ("perm", 24), ("ul", 8), ("al", 6), ("rl", 8), ("ol", 16), ("il", 24), ("dl", 24), ("xl", 24)]
ONCE = {"F": 42, "I": 5, "U": 3}


def lay(items, unit, once):
    at, n = {}, 0
    for i, (k, w) in enumerate(items):
        for r in range(1 if i < once else R + 1):
            at[(k, r)] = n
            n += -(-w // unit) * unit
    return at, n


FA, FN = lay(F32, 8, ONCE["F"])
IA, IN = lay(I32, 8, ONCE["I"])
UA, UN = lay(U16, 16, ONCE["U"])
Q4, U8, BF = "float8_e4m3fn_x4", "uint8", "bfloat16"
SCRATCH = {"F": ("sbuf", [128, FN], "float32"), "I": ("sbuf", [128, IN], "int32"), "U": ("sbuf", [128, UN], "uint16"),
           "jm": ("sbuf", [128, 384], "float32"),
           "pS": ("psum", [128, 1024], "float32"), "pD": ("psum", [128, 2048], "float32"), "pY": ("psum", [128, 1024], "float32")}
for _k, _n in (("X0", 4 * C), ("X1", 4 * C), ("pool", 4 * PW), ("A", 512), ("A64", 4 * TT), ("B", 512), ("ub", 512), ("vb", 512), ("Eb", 2048), ("e1", 128)):
    SCRATCH[_k] = ("sbuf", [128, _n], BF)
for _k, _n in (("x", C), ("u", 128), ("d", 128), ("v", 128), ("w", 512), ("e", 512), ("b", 128), ("a0", 224), ("a1", 224), ("a2", 224)):
    SCRATCH["q" + _k] = ("sbuf", [128, _n], Q4)
    SCRATCH["s" + _k] = ("sbuf", [128, _n], U8)
SEMAPHORES = ["cv", "cs", "ct", "cg", "sent"] + ["arr%d" % t for t in range(R)] + ["d%d" % i for i in range(24)]
ORDER = []


def arrange(ops, deps, last):
    n = len(ops)
    after = [[] for _ in ops]
    for i, d in enumerate(deps):
        for j in d:
            after[j].append(i)

    def span(w, kind, G):
        return G[1] + w[2] if kind == "d" else w[2] * G[3 + w[4]]

    def gap(i, j, G):
        return G[0] + (G[2] if ops[i][3] == "r" and ops[j][3] == "w" else 0.0)

    def replay(seq, way, G):
        free, end = {q: 0.0 for q in "vstgy"}, [0.0] * n
        for i in seq:
            w = ops[i][0][way[i]]
            s = max([free[w[0]]] + [end[j] + gap(j, i, G) for j in deps[i]] + ([end[last[w[3]]] + G[0]] if w[3] else []))
            end[i] = s + span(w, ops[i][3], G)
            free[w[0]] = s + 60 if ops[i][3] == "d" else end[i]
        return max(end)

    G = GUESS[0]
    base = [min(span(w, ops[i][3], G) for w in ops[i][0]) for i in range(n)]
    gaps = [[(j, gap(i, j, G)) for j in after[i]] for i in range(n)]

    def greedy(more, lean, step):
        road = [0.0] * n
        for i in range(n - 1, -1, -1):
            road[i] = base[i] + more[i] + max([t + road[j] for j, t in gaps[i]] + [0.0])
        free = {q: 0.0 for q in "vstgy"}
        end, way, seq, left, t0 = {}, {}, [], [len(d) for d in deps], [0.0] * n
        ready = [i for i in range(n) if not deps[i]]
        while ready:
            best = None
            for i in ready:
                pick = None
                for k, w in enumerate(ops[i][0]):
                    if w[3] and last[w[3]] not in end:
                        continue
                    s = max(t0[i], free[w[0]], end[last[w[3]]] + G[0] if w[3] else 0.0)
                    f = s + w[2] + (lean[i] + w[2] if w[0] == "v" else 0.0)
                    if pick is None or f < pick[2]:
                        pick = (s, k, f)
                key = (int(pick[0] / step), -road[i])
                if best is None or key < best[0]:
                    best = (key, i, pick)
            i, (s, k, f) = best[1], best[2]
            ready.remove(i)
            w = ops[i][0][k]
            way[i], end[i] = k, s + span(w, ops[i][3], G)
            free[w[0]] = s + 60 if ops[i][3] == "d" else end[i]
            seq.append(i)
            for j in after[i]:
                t0[j] = max(t0[j], end[i] + gap(i, j, G))
                left[j] -= 1
                if left[j] == 0:
                    ready.append(j)
        return sum(replay(seq, way, H) for H in GUESS), seq, way

    z = [12345]
    two = [i for i in range(n) if len(ops[i][0]) > 1]

    def draw():
        z[0] = (z[0] * 1103515245 + 12345) % 2147483648
        return z[0] / 2147483648

    more, lean, step = [0.0] * n, [100.0] * n, 30
    best = greedy(more, lean, step)
    for _ in range(TRIES):
        m2, l2 = list(more), list(lean)
        for _ in range(8):
            m2[int(draw() * n)] = 1000 * (draw() - 0.3)
            l2[two[int(draw() * len(two))]] = 1200 * draw() - 500
        s2 = step if draw() < 0.8 else 10 + 150 * draw()
        got = greedy(m2, l2, s2)
        if got[0] <= best[0]:
            best, more, lean, step = got, m2, l2, s2
    return best[1], best[2]


def rank_program(g, core, T, topo):
    rank = T.rank_of(core)
    if rank is None:
        return
    odd = bin(rank).count("1") % 2 == 1
    ops = []
    now = [0]

    def v(name, a=0, b=None, s=1, r=None):
        for at, items, buf in ((FA, F32, "F"), (IA, I32, "I"), (UA, U16, "U")):
            if (name, 0) in at:
                o = at.get((name, now[0] if r is None else r), at[(name, 0)])
                return (buf, o + a, o + (dict(items)[name] if b is None else b), s, None, None)
        return (name, a, SCRATCH[name][1][1] if b is None else b, s, None, None)

    def ind(w, o):
        return w[:4] + (o, w[5])

    def bits(w, d):
        return w[:5] + (d,)

    def ap(w):
        if not isinstance(w, tuple):
            return w
        n, a, b, s, o, c = w
        x = T[n][:, a:b:s] if s > 0 else T[n][:, b - 1:(a - 1 if a else None):s]
        if c is not None:
            x = x.bitcast(c)
        if o is not None:
            x = x.indirect(ap(o))
        return x

    def cols(w):
        if not isinstance(w, tuple):
            return set()
        n, a, b, s, o, c = w
        if SCRATCH[n][0] == "psum":
            return {(n, a // 512)}
        r = {(n, j) for j in range(a, b, abs(s))}
        return r | cols(o) if o is not None else r

    def width(w):
        return 16 * width(w[4]) if w[4] is not None else len(range(w[1], w[2], abs(w[3])))

    def way(q, fn, o, ins, c, more=None):
        ins = [w for w in ins if isinstance(w, tuple)]
        if o[4] is not None:
            return (q, fn, 50 + 3.2 * width(o), more, 2)
        if any(w[4] is not None for w in ins):
            return (q, fn, 55 + 1.3 * width(o), more, 1)
        return (q, fn, 1.04 * max(64, c * max(width(w) for w in ins + [o])), more, 0)

    def put(ways, outs, ins, kind="c"):
        rd, wr = set(), set()
        for w in ins:
            rd |= cols(w)
        for w in outs:
            wr |= cols(w[:4] + (None, None))
            if w[4] is not None:
                rd |= cols(w[4])
        ops.append((ways, rd, wr, kind, {c for c in rd if SCRATCH[c[0]][0] == "psum"}))

    def kinds(ws, *ds):
        return all(SCRATCH[w[0]][2] in ds for w in ws)

    def way_act(o, i, f, bias, scale, more=None, acc=None):
        kw = {}
        if bias != 0.0:
            kw["bias"] = ap(bias)
        if scale != 1.0:
            kw["scale"] = ap(scale)
        if acc is not None:
            kw["accum_out"] = ap(acc)
        return way("s", lambda: g.scalar.activation(ap(o), ap(i), f, **kw), o, [i], 1, more)

    def lin(o, i, scale=1.0, bias=0.0, on="vs"):
        ways = []
        c = 0.5 if kinds([o, i], BF) else 1
        if "v" in on:
            if scale == 1.0 and bias == 0.0:
                ways.append(way("v", lambda: g.vector.tensor_copy(ap(o), ap(i)), o, [i], c))
            else:
                ways.append(way("v", lambda: g.vector.tensor_scalar(ap(o), ap(i), ap(scale), ap(bias), OP.mult, OP.add), o, [i], c))
        if "s" in on and kinds([o, i], BF, "float32") and o[4] is None:
            ways.append(way_act(o, i, AF.Copy if bias == 0.0 and not isinstance(scale, tuple) else AF.Identity, bias, scale))
        put(ways, [o], [i, bias, scale])

    def way_iota(o, pat, base, cm):
        kw = {} if o[0] == "I" else {"allow_small_or_imprecise_dtypes": True}
        return ("g", lambda: g.iota(ap(o), pat, base, cm, **kw), 130 + 2.1 * width(o), None, 0)

    def fill(o, c):
        ways = [way("v", lambda: g.vector.memset(ap(o), c), o, [], 1)]
        ways.append(way_act(o, v("jm", 0, width(o)), AF.Identity, float(c), 0.0, ("jm", 0)))
        if c == int(c) and abs(c) < 2 ** 24 and o[3] == 1:
            ways.append(way_iota(o, [[0, width(o)]], int(c), 0))
        put(ways, [o], [])

    def tt(o, a, b, op):
        c = 1 if SCRATCH[a[0]][0] == "psum" else 2
        put([way("v", lambda: g.vector.tensor_tensor(ap(o), ap(a), ap(b), op), o, [a, b], c)], [o], [a, b])

    def ts(o, a, s1, op0, s2=None, op1=None):
        if op1 is None:
            put([way("v", lambda: g.vector.tensor_scalar(ap(o), ap(a), ap(s1), None, op0), o, [a], 1)], [o], [a, s1])
        else:
            put([way("v", lambda: g.vector.tensor_scalar(ap(o), ap(a), ap(s1), ap(s2), op0, op1), o, [a], 1)], [o], [a, s1, s2])

    def scan(o, a, b, op0, op1, init=0.0):
        put([way("v", lambda: g.vector.tensor_tensor_scan(ap(o), ap(a), ap(b), init, op0, op1), o, [a], 1)], [o], [a, b])

    def quant(q, s, i):
        put([("v", lambda: g.vector.quantize_mx(ap(q), ap(s), ap(i)), 15 + 0.28 * width(i), None, 0)], [q, s], [i])

    def act(o, i, f, bias=0.0, scale=1.0, acc=None):
        put([way_act(o, i, f, bias, scale, None, acc)], [o] + ([acc] if acc else []), [i, bias, scale])

    def mm(o, wq, ws, xq, xs):
        put([("t", lambda: g.tensor.matmul_mx(ap(o), ap(wq), ap(ws), ap(xq), ap(xs), True, True), 0.8 * (width(o) + 16), None, 0)], [o], [wq, ws, xq, xs])

    def iota(o, pat, base, cm=0):
        put([way_iota(o, pat, base, cm)], [o], [])

    def dma(q, fn, outs, ins, more=0.0):
        put([(q, fn, more, None, 0)], outs, ins, "d")

    dma("y", lambda: g.sync.dma_start(ap(v("sz")), T.sz[:]), [v("sz")], [])
    dma("s", lambda: g.scalar.dma_start(T.ub[:], T.u[:]), [v("ub")], [], 600)
    dma("y", lambda: g.sync.dma_start(T.X0[:], T.x[:]), [v("X0")], [], 2000)
    dma("y", lambda: g.sync.dma_start(T.qw[:].bitcast(dt.uint8), T.wc[:]), [v("qw")], [v("X0", 0, 1)], 1300)
    dma("y", lambda: g.sync.dma_start(T.sw[:], T.ws[:]), [v("sw")], [v("X0", 0, 1)], 300)
    dma("y", lambda: g.sync.dma_start(T.vb[:], T.v[:]), [v("vb")], [v("X0", 0, 1)], 600)

    order = [2, 1, 0] if odd else [0, 1, 2]
    iota(v("pc"), [[0, 1]], 0, 1)
    iota(v("jm"), [[0, 24], [1, 16]], 0)
    iota(v("iota"), [[1, 480]], 0)
    iota(v("i1"), [[0, 8], [1, 4]], 1)
    iota(v("e1"), [[0, 128]], 1)
    iota(v("levi"), [[1, 4], [0, 8]], 0)
    iota(v("thr", 0, 6), [[order[1] - order[0], 3], [0, 2]], order[0])
    ts(v("ri"), v("pc"), 15, OP.bitwise_and)
    lin(v("rcol"), v("ri"))
    ts(v("mask"), v("jm"), v("rcol"), OP.is_equal)
    act(v("seg"), v("jm"), AF.Sign)
    fill(v("one"), -1.0)
    iota(v("crep", 0, 80), [[0, 2], [4, 8], [-1, 5]], 4)
    lin(v("pit", 1, 81), v("crep", 0, 80), 1.0, -1.0)
    fill(v("crep", 4, 80, 5), 0.0)
    fill(v("crep", 80, 96), 0.0)
    iota(v("crep", 96, 160), [[40, 2], [0, 4], [5, 8]], 4)
    for h in range(2):
        fill(v("crep", 120 + 32 * h, 123 + 32 * h), 89.0 + 9 * h)
        fill(v("crep", 123 + 32 * h, 128 + 32 * h), 80.0)
    iota(v("crep", 161, 179), [[0, 2], [5, 9]], 4)
    fill(v("crep", 160, 179, 9), 4.0)
    fill(v("crep", 179, 192), 4.0)
    tt(v("cmsk"), v("crep"), v("mask", 0, 192), OP.mult)
    scan(v("cscan"), v("seg", 0, 192), v("cmsk"), OP.mult, OP.add)
    lin(v("cl", 0, 12), v("cscan", 15, 192, 16))
    ts(v("r1"), v("pc"), 1, OP.bitwise_and)
    lin(v("cl", 12, 13), v("r1"), 1.0, 6.0)
    lin(v("cl", 14, 15), v("r1"), 16.0, 15.0)
    L80, L48, LK, LP, LN, LE = v("cl", 0, 5), v("cl", 0, 3), v("cl", 6, 10), v("cl", 10, 12), v("cl", 12, 13), v("cl", 14, 15)
    lin(v("qh"), v("iota", 0, 32, 16), 1.0, v("rcol"))
    lin(v("jd"), v("iota", 0, 384, 16), 1.0, v("rcol"))
    lin(v("dum", 0, 6), v("jd", 0, 6), 1.0, float(ZERO))
    lin(v("dum", 6, 8), v("qh"), 1.0, 384.0)
    fill(v("dum", 8, 16), 384.0)
    fill(v("thr", 6, 16), 0.0)
    lin(v("ev"), v("iota", 0, 32), 512.0, 703.5)
    fill(v("nq"), 1.0)
    for h in range(2):
        ts(v("pq", 40 * h, 40 * h + 40), v("pit", 1, 41), v("qh", h, h + 1), OP.subtract, 64.0, OP.add)
        lin(v("nq", 1 + 9 * h, 9 + 9 * h), v("one", 0, 8), v("qh", h, h + 1))
        lin(v("lev", 32 * h, 32 * h + 24), v("levi", 0, 24), -32 * KEY, BASE[h] - 31 * KEY - 1 + PAD)
        fill(v("lev", 32 * h + 27, 32 * h + 32), BASE[h] + ZERO)
    fill(v("pq", 4, 80, 5), 31.0)
    fill(v("pit", 0, 81, 5), 0.0)
    tt(v("dP"), v("pit", 1, 41), v("pit", 0, 40), OP.subtract)
    fill(v("pat"), 9e29)
    fill(v("pat", 0, 40, 5), -9e29)
    fill(v("big"), 9e29)
    fill(v("p9"), 0.0)
    fill(v("p9", 0, 18, 9), STAY)
    fill(v("S", 384, 392), -1e29)
    fill(v("A", 384, 512), 0.0)
    fill(v("B", 384, 512), 0.0)
    for b in range(4):
        fill(v("pool", PW * b + ZERO, PW * b + PW), 0.0)
    ts(v("pi"), v("jd"), 1.0 / 24, OP.mult, -0.5 + 1.0 / 48, OP.add)
    lin(v("a5", r=R), v("jd"), 16.0)
    lin(v("y", r=R), v("pi"), -383.0)
    tt(v("x", r=R), v("a5", r=R), v("y", r=R), OP.add)
    lin(v("perm"), v("x", r=R))
    fill(v("lst", 0, 368), 0.0)
    fill(v("Rr", 0, 1), 0.0)
    fill(v("En", 0, 1), PAD)
    lin(v("sub", 0, 6), v("thr", 0, 6), 1.0, 1.0)
    fill(v("sub", 8, 16), 1.0)
    fill(v("Mn", 0, 1), -9e29)
    fill(v("Cw", 0, 1), WHOLE)
    for t in range(R):
        fill(v("N", 0, 384, r=t), 0.0)
    for b in range(8):
        fill(v("Eb", 256 * b, 256 * b + 256), 0.0)
    for b in range(4):
        o = v("Eb", 512 * b + b, 512 * b + 512, 4)
        put([("g", lambda o=o: g.affine_select(ap(o), T.e1[:], [[-1, 128]], OP.is_equal, 0.0, 0, 1), 440, None, 0)], [o], [v("e1")])
        if b % 2:
            quant(v("qe", 128 * b - 128, 128 * b + 128), v("se", 128 * b - 128, 128 * b + 128), v("Eb", 512 * b - 512, 512 * b + 512))
    quant(v("qv"), v("sv"), v("vb"))
    quant(v("qu"), v("su"), v("ub"))
    lin(v("ul"), v("iota", 0, 128, 16))
    lin(bits(v("qd"), dt.uint32), ind(bits(v("qu"), dt.uint32), v("ul")))
    act(v("sd"), ind(v("su"), v("ul")), AF.Copy)

    def state(n):
        lin(v("rl", 0, n), v("lst", 0, n))
        lin(v("sub", 6, 8), v("lst", 0, 2))
        lin(v("Rr", 1, 1 + 16 * n), ind(v("iota"), v("rl", 0, n)))
        scan(v("En", 2, 34), v("Rr", 1, 33), v("Rr", 1, 33), OP.add, OP.max)
        tt(v("em"), v("En", 2, 34), v("mask", 0, 32), OP.mult)
        scan(v("es"), v("seg", 0, 32), v("em"), OP.mult, OP.add)
        tt(v("inv"), ind(v("sub"), LN), v("thr"), OP.is_le)
        tt(v("pos"), ind(v("es"), LE), v("sub"), OP.subtract)
        tt(v("tt"), v("inv"), v("dum"), OP.mult)
        tt(v("off"), v("pos"), v("tt"), OP.max)
        lin(v("ol"), v("off"))

    def ahead():
        nw = v("Rr", 0, 40)
        tt(v("w"), ind(nw, L80), v("pq"), OP.add)
        ts(v("w2"), v("w"), 31, OP.bitwise_and)
        tt(v("km"), ind(nw, L80), v("w2"), OP.subtract)
        lin(v("kt"), v("km"), KEY)
        tt(v("Vk", 1, 81), ind(v("En", 0, 34), L80), v("kt"), OP.add)
        tt(v("dK"), v("Vk", 0, 80), v("Vk", 1, 81), OP.subtract)
        act(v("kp0"), v("off", 0, 6), AF.Relu, bias=float(ZERO), scale=-1.0)
        for a in range(6):
            o = 32 * (a % 2) + 24 + a // 2
            lin(v("lev", o, o + 1), v("kp0", a, a + 1), -1.0, BASE[a % 2] + 1024.0 * (3 - order[a // 2]) - STAY + ZERO, on="s")
        tt(v("NF", 1, 33), v("Rr", 1, 33), v("i1"), OP.add)
        lin(v("VF", 1, 49), ind(v("NF", 0, 33), L48), -1.0 / 32)
        tt(v("dF"), v("VF", 0, 40), v("VF", 1, 41), OP.subtract)
        lin(ind(v("N"), v("ol", 6, 8)), v("ev"))
        scan(v("es2"), v("one"), v("N", 0, 384), OP.add, OP.max)
        lin(v("ep"), ind(v("es2"), v("perm")), on="s")
        o, i = v("enc"), v("ep")
        dma("y", lambda: g.sync.dma_start(ap(o), T.F[0:128:16, i[1]:i[2]]), [o], [i])
        lin(v("pm"), v("enc"), 1.0 / 512, WHOLE)
        lin(v("p1"), v("pm"), 1.0, -WHOLE)
        lin(v("pf"), v("pm"), 1.0, -WHOLE - 1)
        lin(v("a5"), v("p1"), 512.0, 192.5)
        tt(v("yp"), v("a5"), v("enc"), OP.subtract)
        lin(v("kf"), v("yp"), 1.0, -1.0)
        lin(v("y0"), v("pf"), 1.0, -15.5)
        tt(v("y"), v("yp"), v("y0"), OP.add)
        lin(v("lm"), v("y"), 1.0 / 32, WHOLE)
        lin(v("l0"), v("lm"), 1.0, -WHOLE)
        lin(v("l32"), v("l0"), 32.0, -55.5)
        tt(v("q40"), v("y"), v("l32"), OP.subtract)
        tt(v("kq"), v("l32"), v("pf"), OP.subtract)
        for m in range(8):
            lin(v("KQ", m, 192, 8), v("kq"), 1.0 / 32, (4 * m + 54.5) / 32 + HALF - 128)

    def scores(X, o, wq, ws):
        for h in range(2):
            q, s = v("qx", 192 * h, 192 * h + 192), v("sx", 192 * h, 192 * h + 192)
            quant(q, s, v(X, 768 * h, 768 * h + 768))
            mm(v(o, 512 * h, 512 * h + 192), wq, ws, q, s)

    lin(v("lst", 0, 2), v("sz"))
    state(2)
    far = []
    for t in range(R):
        now[0] = t
        X = "X%d" % min(t, 1)
        qa, sa = "qa%d" % t, "sa%d" % t
        ahead()
        scores(X, "pS", v("qd"), v("sd"))
        for h in range(2):
            lin(v("S", 192 * h, 192 * h + 192), v("pS", 512 * h, 512 * h + 192))
        for b in range(4):
            lin(v("pool", PW * b, PW * b + C), v(X, b, 4 * C, 4), 64.0, on="s")
        lin(v("Mn", 1, 33), ind(v("S"), v("ol", 8, 10)))
        lin(v("M5"), ind(v("Mn", 0, 33), L48))
        scan(v("Sf"), v("pat"), v("M5", 0, 40), OP.min, OP.max)
        tt(v("u"), v("M5", 0, 40), v("Sf"), OP.is_lt)
        scan(v("DP"), v("dP"), v("u"), OP.add, OP.mult)
        scan(v("DF"), v("dF"), v("u"), OP.add, OP.mult)
        for h in range(2):
            scan(v("D", 40 * h, 40 * h + 40), v("dK", 40 * h, 40 * h + 40), v("u"), OP.add, OP.mult)
        tt(v("ne"), ind(v("DP"), LP), v("nq"), OP.not_equal)
        scan(v("D", 81, 99), v("ne", 0, 18), v("p9", 0, 18), OP.mult, OP.max)
        tt(v("cand"), ind(v("D", 0, 99), LK), v("lev"), OP.add)
        at = [64 * order.index(i) for i in range(3)]
        scan(v("T3", at[0], at[0] + 64), v("cand"), v("big", 0, 64), OP.max, OP.min)
        for i in (1, 2):
            scan(v("T3", at[i] + i, at[i] + 64), v("cand", i, 64), v("T3", at[i - 1] + i - 1, at[i - 1] + 63), OP.max, OP.min)
        lin(v("Ti"), v("T3", 31, 192, 32))
        ts(v("Ta"), v("Ti"), 1023, OP.bitwise_and)
        lin(v("al"), v("Ta"))
        for b in range(4):
            lin(v("A", b, 4 * TT, 4), ind(v("pool", PW * b, PW * b + PW), v("al")), 1.0 / 64, on="vvss"[b])
        quant(v(qa, 96, 224), v(sa, 96, 224), v("A"))
        mate = T.cores[rank ^ (1 << t)]
        rid, pid, _ = topo.addr(mate)
        to = (T.sem["arr%d" % t], T.sem.sent, pid, rid, topo.mask(core, mate))
        far.append(2 * len(topo.engines(core, mate)))
        put([("g", lambda qa=qa, to=to: g.remote_dma(T[qa][:, 0:96].bitcast(dt.uint8), T[qa][:, 96:192].bitcast(dt.uint8), *to), 400, None, 0)], [], [v(qa, 96, 192)], "r")
        put([("g", lambda sa=sa, to=to: g.remote_dma(T[sa][:, 0:96], T[sa][:, 96:192], *to), 400, None, 0)], [], [v(sa, 96, 192)], "r")
        lin(v("A64"), v("A", 0, 4 * TT), 64.0, on="s")
        lin(v("cx"), v("D", 4, 80, 5), 1.0 / (32 * KEY), WHOLE)
        lin(v("fg"), v("D", 89, 99, 9), 1.0 / STAY)
        lin(v("cc"), v("D", 89, 99, 9), -1.0 / STAY, 1.0)
        for h in range(2):
            arr, fg, n0 = v("arr", h, h + 1), v("fg", h, h + 1), v("sub", 6 + h, 7 + h)
            act(v("cs", 8 * h, 8 * h + 8), v("cx", 8 * h, 8 * h + 8), AF.Identity, bias=-WHOLE, acc=arr)
            lin(v("lst", h, h + 1), n0, fg, arr)
            lin(v("lst", 2 + h, 3 + h), n0, fg)
            lin(v("lst", 5 + h, 6 + h), v("cc", h, h + 1), 1.0, arr)
        now[0] = t + 1
        state(7)
        scan(v("En", 40, 72), v("Rr", 33, 65), v("Rr", 80, 112), OP.add, OP.add, -8.0)
        if t == R - 1:
            a = v("Rr")[1] + 1
            dma("y", lambda a=a: g.sync.dma_start(T.oz[:], T.F[0:128:16, a:a + 32]), [], [v("Rr", 1, 33)])
        now[0] = t
        for m in range(8):
            act(v("RL", m, 192, 8), v("yp"), AF.Relu, bias=v("DF", 5 * m + 4, 5 * m + 5), scale=1.0 / 32)
            act(v("AB", m, 192, 8), v("pf"), AF.Abs, bias=v("DP", 5 * m + 4, 5 * m + 5))
        act(v("EQ"), v("AB"), AF.Relu, bias=1032.0, scale=-1032.0)
        tt(v("fw"), v("KQ"), v("RL"), OP.subtract)
        scan(v("Cw", 1, 193), v("fw"), v("EQ"), OP.add, OP.add, WHOLE)
        tt(v("W"), v("Cw", 8, 200, 8), v("Cw", 0, 192, 8), OP.subtract)
        lin(v("Wb"), v("W"), 100.0, 100.0)
        lin(v("nW"), v("W"), -1.0)
        tt(v("cd"), v("Wb"), v("q40"), OP.min)
        tt(v("idx"), v("cd"), v("p1"), OP.max)
        lin(v("il"), v("idx"))
        tt(v("x"), v("nW"), v("kf"), OP.min)
        tt(v("t3"), v("W"), v("x"), OP.max)
        tt(v("lk"), ind(v("En"), v("il")), v("mask"), OP.mult)
        scan(v("ls"), v("seg"), v("lk"), OP.mult, OP.add)
        tt(v("d"), v("ls", 15, 384, 16), v("t3"), OP.add)
        lin(v("dl"), v("d"))
        lin(ind(v("O"), v("dl")), v("iota", 0, 384))
        lin(ind(v("O"), v("ol", 0, 6, r=t + 1)), v("iota", 384, 480))
        for r in range(16):
            lin(v("om", r, 384, 16), v("O", r, 384, 16), v("mask", r, r + 1))
        scan(v("os"), v("seg"), v("om"), OP.mult, OP.add)
        lin(v("xl"), v("os", 15, 384, 16))
        put([("t", lambda sem=to[0], n=far[-1]: g.tensor.wait_ge(sem, n), 0, None, 0)], [v(qa, 0, 96), v(sa, 0, 96)], [], "w")
        for b in range(4):
            mm(v("pD", 512 * b, 512 * b + 128), v("qe", 128 * b, 128 * b + 128), v("se", 128 * b, 128 * b + 128), v(qa, 0, 128), v(sa, 0, 128))
            tt(v("B", b, 4 * TT, 4), v("pD", 512 * b, 512 * b + TT, -1), v("A", b, 4 * TT, 4), OP.add)
        quant(v("qb"), v("sb"), v("B"))
        for b in range(4):
            mm(v("pD", 512 * b, 512 * b + 128), v("qw", 128 * b, 128 * b + 128), v("sw", 128 * b, 128 * b + 128), v("qb"), v("sb"))
            tt(v("pool", PW * b + C, PW * b + C + TT), v("pD", 512 * b, 512 * b + TT), v("A64", b, 4 * TT, 4), OP.add)
        for lo in (0, 12):
            for b in range(4):
                lin(v("X1", 64 * lo + b, 64 * lo + 768, 4), ind(v("pool", PW * b, PW * b + PW), v("xl", lo, lo + 12)), 1.0 / 64, on="ssvv"[b])

    scores("X1", "pY", v("qv"), v("sv"))
    for h in range(2):
        q = v("qx", 192 * h, 192 * h + 192)
        dma("y", lambda q=q, h=h: g.sync.dma_start(T.oc[:, 768 * h:768 * h + 768], ap(bits(q, dt.uint8))), [], [q], 500)
        o = v("yo", 192 * h, 192 * h + 192)
        lin(o, v("pY", 512 * h, 512 * h + 192), on="sv"[h])
        dma("s", lambda o=o, h=h: g.scalar.dma_start(T.y[:, 192 * h:192 * h + 192], ap(o)), [], [o], 500)
    for k in range(4):
        dma("y", lambda k=k: g.sync.dma_start(T.osc[4 * k:4 * k + 4, :], T.sx[32 * k:32 * k + 4, :]), [], [v("sx")])

    last, readers, deps, sends = {}, {}, [], []
    for i, (ways, rd, wr, kind, ps) in enumerate(ops):
        d = {last[c] for c in rd | wr if c in last}
        for c in wr | ps:
            d |= readers.get(c, set())
        if kind == "w":
            d |= set(sends[-2:])
        if kind == "r":
            d |= set(sends[-1:])
            sends.append(i)
        deps.append(sorted(d))
        for c in rd:
            readers.setdefault(c, set()).add(i)
        for c in wr:
            last[c] = i
            readers[c] = set()
    if not ORDER:
        ORDER.append(arrange(ops, deps, last))
    seq, pick = ORDER[0]
    ways = {i: ops[i][0][pick[i]] for i in seq}
    place = {i: k for k, i in enumerate(seq)}
    seen, use = {q: {} for q in "vstgy"}, {}
    for i in seq:
        top = {}
        for j in deps[i] + ([last[ways[i][3]]] if ways[i][3] else []):
            if ops[j][3] in "cd":
                k = ways[j][0] if ops[j][3] == "c" else ("d", j)
                if place[j] > place.get(top.get(k), -1):
                    top[k] = j
        s = seen[ways[i][0]]
        use[i] = [j for k, j in top.items() if s.get(k, -1) < place[j]]
        for k, j in top.items():
            s[k] = max(s.get(k, -1), place[j])
    marked = {j for u in use.values() for j in u}
    queue = {"v": g.vector, "s": g.scalar, "t": g.tensor, "g": g, "y": g.sync}
    tick, count, nd = {}, {q: 0 for q in "vstg"}, 0
    for i in seq:
        q, kind = ways[i][0], ops[i][3]
        for j in use[i]:
            queue[q].wait_ge(*tick[j])
        x = ways[i][1]()
        if kind == "c" and i in marked:
            count[q] += 1
            tick[i] = (T.sem["c" + q], count[q])
            x.then_inc(tick[i][0], 1)
        if kind == "d":
            tick[i] = (T.sem["d%d" % nd], 16)
            nd += 1
            x.then_inc(tick[i][0], 16)
    for i in seq:
        if ops[i][3] == "d" and i not in marked:
            g.sync.wait_ge(*tick[i])
    g.wait_ge(T.sem.sent, sum(far))
